import numpy as np
import ml_dtypes


def mxq(x, axis, fmt="e4m3"):
    dtype, down = {"e4m3": (ml_dtypes.float8_e4m3fn, 7), "e5m2": (ml_dtypes.float8_e5m2, 14)}[fmt]
    v = np.moveaxis(np.asarray(x, np.float32).astype(ml_dtypes.bfloat16).astype(np.float64), axis, -1)
    blocks = v.reshape(v.shape[:-1] + (-1, 32))
    amax = np.abs(blocks).max(-1, keepdims=True)
    byte = np.maximum(np.where(amax > 0, np.frexp(amax)[1] - 1 + 127, 0) - down, 1)
    scale = np.exp2(byte - 127.0)
    codes = (blocks / scale).astype(np.float32).astype(dtype).astype(np.float64)
    return np.moveaxis((codes * scale).reshape(v.shape), -1, axis)


WIDE = False


def mx_kscale(k):
    if not WIDE:
        return np.ones(k)
    levels = np.array([10, -10, 5, -5, 0])
    if k % 512:
        return np.exp2(np.random.permutation(np.resize(levels, k // 32))).repeat(32)
    a = np.empty((k // 512, 16))
    for p in range(k // 512):
        a[p, :8] = np.random.permutation(np.resize(levels, 8))
        for g in range(8):
            far = levels[np.abs(levels - a[p, g]) >= 10]
            a[p, g + 8] = far[np.random.randint(len(far))]
    return np.exp2(a.ravel()).repeat(32)


def f64(x):
    return np.asarray(x).astype(np.float64)


def striped(idx):
    return np.tile(np.asarray(idx).reshape(-1, 16).T, (8, 1)).astype(np.uint16)


def unstriped(offs):
    return offs[:16].T.reshape(-1).astype(np.int64)


E2M1 = np.array([0.0, 0.5, 1.0, 1.5, 2.0, 3.0, 4.0, 6.0, -0.0, -0.5, -1.0, -1.5, -2.0, -3.0, -4.0, -6.0])


def pack_weight(w, fmt):
    k, n = w.shape
    w = f64(np.asarray(w, np.float32).astype(ml_dtypes.bfloat16)).reshape(k // 32, 32, n)
    amax = np.abs(w).max(1)
    if fmt == "e4m3":
        byte = np.frexp(amax)[1] - 1 + 127 - 7
    else:
        mant, ex = np.frexp(amax / 6.0)
        byte = np.where(mant > 0.5, ex, ex - 1) + 127
    byte = np.clip(np.where(amax > 0, byte, 1), 1, 254)
    scaled = (w * np.exp2(127.0 - byte)[:, None, :]).reshape(k, n).astype(np.float32)
    by_word = np.ascontiguousarray(scaled.reshape(k // 512, 128, 4, n).transpose(0, 1, 3, 2))
    if fmt == "e4m3":
        words = by_word.astype(ml_dtypes.float8_e4m3fn).view(np.uint8)
    else:
        c = by_word.astype(ml_dtypes.float4_e2m1fn).view(np.uint8) & 0xF
        words = (c[..., 0::2] | (c[..., 1::2] << 4)).reshape(k // 512, 128, 2 * n)
    return np.ascontiguousarray(words), np.ascontiguousarray(byte.astype(np.uint8).reshape(k // 512, 16, n))


def unpack_weight(words, scales, fmt):
    g, _, n = scales.shape
    words = np.ascontiguousarray(words).reshape(g, 128, n, -1)
    if fmt == "e4m3":
        vals = words.view(ml_dtypes.float8_e4m3fn).astype(np.float64)
    else:
        nib = np.empty((g, 128, n, 4), np.uint8)
        nib[..., 0::2] = words & 0xF
        nib[..., 1::2] = words >> 4
        vals = E2M1[nib]
    vals = vals * np.repeat(np.exp2(scales.astype(np.float64) - 127.0), 8, axis=1)[..., None]
    return vals.transpose(0, 1, 3, 2).reshape(g * 512, n)


def sigmoid(v):
    return 1.0 / (1.0 + np.exp(-v))


def bf(x):
    return np.asarray(x, np.float32).astype(ml_dtypes.bfloat16)


def planes(Y):
    r, m = Y.shape
    b = f64(bf(Y)).reshape(r // 32, 32, m)
    amax = np.abs(b).max(1)
    byte = np.clip(np.where(amax > 0, np.frexp(amax)[1] - 1 + 127 - 7, 1), 1, 254)
    codes = (b * np.exp2(127.0 - byte)[:, None, :]).reshape(r, m).astype(np.float32).astype(ml_dtypes.float8_e4m3fn).view(np.uint8)
    words = codes.reshape(r // 512, 128, 4, m).transpose(0, 1, 3, 2)
    return np.ascontiguousarray(words), np.ascontiguousarray(byte.astype(np.uint8).reshape(r // 512, 16, m))


K, T, J, N = 1024, 1024, 512, 512


def setup_inputs():
    n = np.random.standard_normal
    idx = np.random.permutation(T)[:J]
    fk = mx_kscale(K)
    wap = pack_weight(n((K, N)) * 1 / np.sqrt(K) * fk[:, None], "e4m3")
    wgp = pack_weight(n((K, N)) * 1 / np.sqrt(K) * fk[:, None], "e2m1")
    return {
        "xq": (n((K, T)) / fk[:, None]).astype(np.float32),
        "wa_words": wap[0],
        "wa_scales": wap[1],
        "wg_words": wgp[0],
        "wg_scales": wgp[1],
        "res": (1.0 * n((N, T))).astype(np.float32),
        "offs": striped(idx),
    }


def reference(xq, wa_words, wa_scales, wg_words, wg_scales, res, offs):
    idx = unstriped(offs)
    wau = unpack_weight(wa_words, wa_scales, "e4m3")
    wgu = unpack_weight(wg_words, wg_scales, "e2m1")
    xqidxq = mxq(f64(xq)[:, idx], 0, "e4m3")
    p = wau.T @ xqidxq
    g = wgu.T @ xqidxq
    d = p * sigmoid(g)
    dp = np.zeros((N, T))
    dp[:, idx] = d
    y = 0.5 * f64(res) + dp
    words, scales = planes(y)
    return y, words, scales

@@ -1,0 +1,176 @@
+from contextlib import ExitStack
+
+import concourse.mybir as mybir
+
+K, T, J, N = 1024, 1024, 512, 512
+FLOPS = 2 * 2 * K * N * J
+
+F32 = mybir.dt.float32
+BF16 = mybir.dt.bfloat16
+I32 = mybir.dt.int32
+U32 = mybir.dt.uint32
+U16 = mybir.dt.uint16
+U8 = mybir.dt.uint8
+FP8X4 = mybir.dt.float8_e4m3fn_x4
+FP4X4 = mybir.dt.float4_e2m1fn_x4
+ALU = mybir.AluOpType
+ACT = mybir.ActivationFunctionType
+
+P = 128
+PACK = 4
+PASSES = K // (P * PACK)
+HALF = T // 2
+GATE_ROW = 0
+ANSWER_ROW = 4
+
+
+def tile_list_expert_self_gate_pl_kernel(tc, xq, wa_words, wa_scales, wg_words, wg_scales, res, offs, out_0, out_1, out_2):
+    nc = tc.nc
+    with ExitStack() as ctx:
+        keep = ctx.enter_context(tc.tile_pool(name="keep", bufs=1))
+        psum = ctx.enter_context(tc.psum_pool(name="psum", bufs=1))
+
+        offsets = keep.tile([P, J // 16], U16, name="offsets")
+        nc.sync.dma_start(offsets[:], offs)
+
+        scales_raw = keep.tile([P, PASSES, N], U8, name="scales_raw", align_bytes=64)
+        nc.gpsimd.memset(scales_raw[:].bitcast(I32), 0)
+
+        def load_scales(row, src):
+            for q in range(4):
+                nc.sync.dma_start(
+                    out=scales_raw[32 * q + row : 32 * q + row + 4].bitcast(I32),
+                    in_=src[:, 4 * q : 4 * q + 4, :].rearrange("z r c -> r z c").bitcast(I32),
+                )
+
+        pages = [keep.tile([P, T], F32, name=f"page{t}") for t in range(PACK)]
+        for t in range(PACK):
+            nc.vector.memset(pages[t][:], 0.0)
+
+        x_rows = xq.rearrange("(a p i) t -> a p i t", a=PASSES, i=PACK)
+        x_raw = {}
+
+        def load_x(a, u, h, width):
+            piece = keep.tile([P, 2, width], F32, name=f"x_raw{a}{u}{h}")
+            nc.sync.dma_start(out=piece[:], in_=x_rows[a, :, 2 * u : 2 * u + 2, h * HALF : h * HALF + width])
+            for i in range(width // HALF):
+                x_raw[a, u, h + i] = piece[:, :, i * HALF : (i + 1) * HALF]
+
+        wg_raw = keep.tile([P, PASSES, N], U16, name="wg_raw", align_bytes=64)
+        wa_raw = keep.tile([P, PASSES, N], I32, name="wa_raw", align_bytes=64)
+        load_x(0, 0, 0, HALF)
+        load_scales(GATE_ROW, wg_scales)
+        load_x(0, 0, 1, HALF)
+        nc.sync.dma_start(out=wg_raw[:].bitcast(I32), in_=wg_words.rearrange("z p b -> p z b").bitcast(I32))
+        load_x(0, 1, 0, HALF)
+        load_x(0, 1, 1, HALF)
+        load_scales(ANSWER_ROW, wa_scales)
+        for u in range(2):
+            for h in range(2):
+                load_x(1, u, h, HALF)
+        nc.sync.dma_start(out=wa_raw[:], in_=wa_words.rearrange("z p n t -> p z (n t)").bitcast(I32))
+        res_rows = res.rearrange("(p t) c -> p t c", t=PACK)
+        res_sb = [keep.tile([P, T], F32, name=f"res{t}") for t in range(PACK)]
+        for t in range(PACK):
+            nc.sync.dma_start(out=res_sb[t][:], in_=res_rows[:, t, :])
+
+        x_codes = [keep.tile([P, J], U32, name=f"x_codes{a}", align_bytes=64) for a in range(PASSES)]
+        x_scales = [keep.tile([P, J], U8, name=f"x_scales{a}", align_bytes=64) for a in range(PASSES)]
+        wg = keep.tile([P, PASSES, N], U16, name="wg", align_bytes=64)
+        wa = keep.tile([P, PASSES, N], I32, name="wa", align_bytes=64)
+        scales = keep.tile([P, PASSES, N], U8, name="scales", align_bytes=64)
+
+        def round_pair(a, u):
+            pair = keep.tile([P, T * 2], BF16, name=f"pair{a}{u}", align_bytes=64)
+            cols = pair[:].rearrange("p (c e) -> p c e", e=2)
+            for h in range(2):
+                src = x_raw[a, u, h].rearrange("p e c -> p c e")
+                dst = cols[:, h * HALF : (h + 1) * HALF, :]
+                s = {(0, 0, 0): 0, (1, 1, 1): HALF // 2}.get((a, u, h), HALF)
+                if s > 0:
+                    nc.scalar.activation(out=dst[:, :s, :], in_=src[:, :s, :], func=ACT.Copy)
+                if s < HALF:
+                    nc.vector.tensor_copy(out=dst[:, s:, :], in_=src[:, s:, :])
+            return pair
+
+        def deal(dealt, raw):
+            nc.vector.tensor_copy(
+                out=dealt[:].rearrange("p z (t q) -> p z t q", t=PACK), in_=raw[:].rearrange("p z (q t) -> p z t q", t=PACK)
+            )
+
+        for a in range(PASSES):
+            picked = keep.tile([P, 2, J], F32, name=f"picked{a}")
+            for u in range(2):
+                pair = round_pair(a, u)
+                if a == 0:
+                    deal(*((wg, wg_raw), (scales, scales_raw))[u])
+                nc.vector.tensor_copy(out=picked[:, u, :], in_=pair[:].bitcast(F32).indirect(offsets[:]))
+            grouped = keep.tile([P, J * PACK], BF16, name=f"grouped{a}", align_bytes=64)
+            nc.vector.tensor_copy(
+                out=grouped[:].bitcast(F32).rearrange("p (j u) -> p j u", u=2), in_=picked[:].rearrange("p u j -> p j u")
+            )
+            nc.vector.quantize_mx(out=x_codes[a][:].bitcast(FP8X4), scales=x_scales[a][:], in_=grouped[:])
+        nc.vector.tensor_copy(
+            out=wa[:].rearrange("p z (t b i) -> p z b t i", t=PACK, i=4),
+            in_=wa_raw[:].rearrange("p z (b i t) -> p z b t i", t=PACK, i=4),
+        )
+
+        gate_ps = [psum.tile([P, J], F32, name=f"gate_ps{t}") for t in range(PACK)]
+        ans_ps = [psum.tile([P, J], F32, name=f"ans_ps{t}") for t in range(PACK)]
+
+        def product(acc, words, fmt, row, t, a):
+            cols = slice(t * P, (t + 1) * P)
+            nc.tensor.matmul_mx(
+                out=acc[:],
+                lhsT=words[:, a, cols].bitcast(fmt),
+                lhsT_scale=scales[row:P, a, cols],
+                rhs=x_codes[a][:].bitcast(FP8X4),
+                rhs_scale=x_scales[a][:],
+                start=(a == 0),
+                stop=(a == PASSES - 1),
+            )
+
+        for t in range(PACK):
+            product(gate_ps[t], wg, FP4X4, GATE_ROW, t, 0)
+
+        y = {(u, h): keep.tile([P, 2, HALF], F32, name=f"y{u}{h}") for u in range(2) for h in range(2)}
+        y_grouped = [keep.tile([P, HALF, PACK], BF16, name=f"y_grouped{h}", align_bytes=64) for h in range(2)]
+        y_codes = keep.tile([P, T], U32, name="y_codes", align_bytes=64)
+        y_scales = keep.tile([P, T], U8, name="y_scales", align_bytes=64)
+        out_rows = out_0.rearrange("(p t) c -> p t c", t=PACK)
+
+        for t in range(PACK):
+            product(gate_ps[t], wg, FP4X4, GATE_ROW, t, 1)
+            for a in range(PASSES):
+                product(ans_ps[t], wa, FP8X4, ANSWER_ROW, t, a)
+            gate = keep.tile([P, J], F32, name=f"gate{t}")
+            ans = keep.tile([P, J], F32, name=f"ans{t}")
+            nc.scalar.activation(out=gate[:], in_=gate_ps[t][:], func=ACT.Sigmoid)
+            nc.scalar.activation(out=ans[:], in_=ans_ps[t][:], func=ACT.Copy)
+            nc.vector.tensor_tensor(out=pages[t][:].indirect(offsets[:]), in0=ans[:], in1=gate[:], op=ALU.mult)
+            u, e = divmod(t, 2)
+            for h in range(2):
+                cols = slice(h * HALF, (h + 1) * HALF)
+                nc.vector.scalar_tensor_tensor(
+                    out=y[u, h][:, e, :], in0=res_sb[t][:, cols], scalar=0.5, in1=pages[t][:, cols], op0=ALU.mult, op1=ALU.add
+                )
+                nc.sync.dma_start(out=out_rows[:, t, cols], in_=y[u, h][:, e, :])
+            if e == 1:
+                for h in range(2):
+                    src = y[u, h][:].rearrange("p e c -> p c e")
+                    dst = y_grouped[h][:, :, 2 * u : 2 * u + 2]
+                    if u == 1 and h == 1:
+                        nc.vector.tensor_copy(out=dst, in_=src)
+                    else:
+                        nc.scalar.activation(out=dst, in_=src, func=ACT.Copy)
+
+        code_words = out_1.rearrange("z p c r -> p (z c r)").bitcast(I32)
+        for h in (1, 0):
+            cols = slice(h * HALF, (h + 1) * HALF)
+            nc.vector.quantize_mx(
+                out=y_codes[:, cols].bitcast(FP8X4), scales=y_scales[:, cols], in_=y_grouped[h][:].rearrange("p c t -> p (c t)")
+            )
+            nc.sync.dma_start(out=code_words[:, cols], in_=y_codes[:, cols].bitcast(I32))
+        for q in range(4):
+            eng = nc.sync if q % 2 == 0 else nc.scalar
+            eng.dma_start(out=out_2[0, 4 * q : 4 * q + 4, :].bitcast(I32), in_=y_scales[32 * q : 32 * q + 4, :].bitcast(I32))

@@ -20,8 +20,11 @@ P = 128
 PACK = 4
 PASSES = K // (P * PACK)
 HALF = T // 2
+JH = J // 2
+QUARTER = T // 4
 GATE_ROW = 0
 ANSWER_ROW = 4
+SCALAR_SHARE = {(0, 0, 1): 320, (0, 1, 1): 256, (1, 1, 1): 256}
 
 
 def tile_list_expert_self_gate_pl_kernel(tc, xq, wa_words, wa_scales, wg_words, wg_scales, res, offs, out_0, out_1, out_2):
@@ -50,24 +53,20 @@ def tile_list_expert_self_gate_pl_kernel(tc, xq, wa_words, wa_scales, wg_words, 
         x_rows = xq.rearrange("(a p i) t -> a p i t", a=PASSES, i=PACK)
         x_raw = {}
 
-        def load_x(a, u, h, width):
-            piece = keep.tile([P, 2, width], F32, name=f"x_raw{a}{u}{h}")
-            nc.sync.dma_start(out=piece[:], in_=x_rows[a, :, 2 * u : 2 * u + 2, h * HALF : h * HALF + width])
-            for i in range(width // HALF):
-                x_raw[a, u, h + i] = piece[:, :, i * HALF : (i + 1) * HALF]
+        def load_x(a, u, h):
+            x_raw[a, u, h] = keep.tile([P, 2, HALF], F32, name=f"x_raw{a}{u}{h}")
+            nc.sync.dma_start(out=x_raw[a, u, h][:], in_=x_rows[a, :, 2 * u : 2 * u + 2, h * HALF : (h + 1) * HALF])
 
         wg_raw = keep.tile([P, PASSES, N], U16, name="wg_raw", align_bytes=64)
         wa_raw = keep.tile([P, PASSES, N], I32, name="wa_raw", align_bytes=64)
-        load_x(0, 0, 0, HALF)
-        load_scales(GATE_ROW, wg_scales)
-        load_x(0, 0, 1, HALF)
         nc.sync.dma_start(out=wg_raw[:].bitcast(I32), in_=wg_words.rearrange("z p b -> p z b").bitcast(I32))
-        load_x(0, 1, 0, HALF)
-        load_x(0, 1, 1, HALF)
+        load_x(0, 0, 0)
+        load_scales(GATE_ROW, wg_scales)
+        load_x(0, 0, 1)
         load_scales(ANSWER_ROW, wa_scales)
-        for u in range(2):
+        for a, u in ((0, 1), (1, 0), (1, 1)):
             for h in range(2):
-                load_x(1, u, h, HALF)
+                load_x(a, u, h)
         nc.sync.dma_start(out=wa_raw[:], in_=wa_words.rearrange("z p n t -> p z (n t)").bitcast(I32))
         res_rows = res.rearrange("(p t) c -> p t c", t=PACK)
         res_sb = [keep.tile([P, T], F32, name=f"res{t}") for t in range(PACK)]
@@ -77,100 +76,158 @@ def tile_list_expert_self_gate_pl_kernel(tc, xq, wa_words, wa_scales, wg_words, 
         x_codes = [keep.tile([P, J], U32, name=f"x_codes{a}", align_bytes=64) for a in range(PASSES)]
         x_scales = [keep.tile([P, J], U8, name=f"x_scales{a}", align_bytes=64) for a in range(PASSES)]
         wg = keep.tile([P, PASSES, N], U16, name="wg", align_bytes=64)
-        wa = keep.tile([P, PASSES, N], I32, name="wa", align_bytes=64)
+        wa = keep.tile([P, PACK, PASSES, P], I32, name="wa", align_bytes=64)
         scales = keep.tile([P, PASSES, N], U8, name="scales", align_bytes=64)
+        for dealt, raw in ((wg, wg_raw), (scales, scales_raw)):
+            nc.vector.tensor_copy(
+                out=dealt[:].rearrange("p z (t q) -> p z t q", t=PACK), in_=raw[:].rearrange("p z (q t) -> p z t q", t=PACK)
+            )
 
         def round_pair(a, u):
             pair = keep.tile([P, T * 2], BF16, name=f"pair{a}{u}", align_bytes=64)
             cols = pair[:].rearrange("p (c e) -> p c e", e=2)
             for h in range(2):
-                src = x_raw[a, u, h].rearrange("p e c -> p c e")
+                src = x_raw[a, u, h][:].rearrange("p e c -> p c e")
                 dst = cols[:, h * HALF : (h + 1) * HALF, :]
-                s = {(0, 0, 0): 0, (1, 1, 1): HALF // 2}.get((a, u, h), HALF)
-                if s > 0:
-                    nc.scalar.activation(out=dst[:, :s, :], in_=src[:, :s, :], func=ACT.Copy)
+                s = SCALAR_SHARE.get((a, u, h), HALF)
+                nc.scalar.activation(out=dst[:, :s, :], in_=src[:, :s, :], func=ACT.Copy)
                 if s < HALF:
                     nc.vector.tensor_copy(out=dst[:, s:, :], in_=src[:, s:, :])
-            return pair
+            return pair[:].bitcast(F32)
 
-        def deal(dealt, raw):
+        def gather(picked, u, window, j0, j1):
+            nc.vector.tensor_copy(out=picked[:, u, j0:j1], in_=window.indirect(offsets[:, j0 // 16 : j1 // 16]))
+
+        def weave(grouped, picked, j0, j1):
             nc.vector.tensor_copy(
-                out=dealt[:].rearrange("p z (t q) -> p z t q", t=PACK), in_=raw[:].rearrange("p z (q t) -> p z t q", t=PACK)
+                out=grouped[:, PACK * j0 : PACK * j1].bitcast(F32).rearrange("p (j u) -> p j u", u=2),
+                in_=picked[:, :, j0:j1].rearrange("p u j -> p j u"),
             )
 
-        for a in range(PASSES):
-            picked = keep.tile([P, 2, J], F32, name=f"picked{a}")
-            for u in range(2):
-                pair = round_pair(a, u)
-                if a == 0:
-                    deal(*((wg, wg_raw), (scales, scales_raw))[u])
-                nc.vector.tensor_copy(out=picked[:, u, :], in_=pair[:].bitcast(F32).indirect(offsets[:]))
-            grouped = keep.tile([P, J * PACK], BF16, name=f"grouped{a}", align_bytes=64)
-            nc.vector.tensor_copy(
-                out=grouped[:].bitcast(F32).rearrange("p (j u) -> p j u", u=2), in_=picked[:].rearrange("p u j -> p j u")
+        def quantize(a, grouped, j0, j1):
+            nc.vector.quantize_mx(
+                out=x_codes[a][:, j0:j1].bitcast(FP8X4), scales=x_scales[a][:, j0:j1], in_=grouped[:, PACK * j0 : PACK * j1]
             )
-            nc.vector.quantize_mx(out=x_codes[a][:].bitcast(FP8X4), scales=x_scales[a][:], in_=grouped[:])
+
+        picked = [keep.tile([P, 2, J], F32, name=f"picked{a}") for a in range(PASSES)]
+        grouped = [keep.tile([P, J * PACK], BF16, name=f"grouped{a}", align_bytes=64) for a in range(PASSES)]
+        for u in range(2):
+            gather(picked[0], u, round_pair(0, u), 0, J)
+        weave(grouped[0], picked[0], 0, J)
+        quantize(0, grouped[0], 0, J)
+        gather(picked[1], 0, round_pair(1, 0), 0, J)
+        last = round_pair(1, 1)
+        halves = ((0, JH), (JH, J))
+        for j0, j1 in halves:
+            gather(picked[1], 1, last, j0, j1)
+        for j0, j1 in halves:
+            weave(grouped[1], picked[1], j0, j1)
+        quantize(1, grouped[1], 0, JH)
+        nc.vector.tensor_copy(out=wa[:, 0], in_=wa_raw[:].rearrange("p z (q t) -> p t z q", t=PACK)[:, 0])
+        quantize(1, grouped[1], JH, J)
         nc.vector.tensor_copy(
-            out=wa[:].rearrange("p z (t b i) -> p z b t i", t=PACK, i=4),
-            in_=wa_raw[:].rearrange("p z (b i t) -> p z b t i", t=PACK, i=4),
+            out=wa[:, 1:].rearrange("p t z (b i) -> p z b t i", i=4),
+            in_=wa_raw[:].rearrange("p z (b i t) -> p z b t i", t=PACK, i=4)[:, :, :, 1:, :],
         )
 
-        gate_ps = [psum.tile([P, J], F32, name=f"gate_ps{t}") for t in range(PACK)]
-        ans_ps = [psum.tile([P, J], F32, name=f"ans_ps{t}") for t in range(PACK)]
+        def product(acc, gate, t, a, j0, j1):
+            width = P if gate and j1 - j0 < J else j1 - j0
+            for c in range(j0, j1, width):
+                nc.tensor.matmul_mx(
+                    out=acc[:, c - j0 : c - j0 + width],
+                    lhsT=wg[:, a, t * P : (t + 1) * P].bitcast(FP4X4) if gate else wa[:, t, a, :].bitcast(FP8X4),
+                    lhsT_scale=scales[(GATE_ROW if gate else ANSWER_ROW) : P, a, t * P : (t + 1) * P],
+                    rhs=x_codes[a][:, c : c + width].bitcast(FP8X4),
+                    rhs_scale=x_scales[a][:, c : c + width],
+                    start=(a == 0 and c == j0),
+                    stop=(a == PASSES - 1 and c + width == j1),
+                )
 
-        def product(acc, words, fmt, row, t, a):
-            cols = slice(t * P, (t + 1) * P)
-            nc.tensor.matmul_mx(
-                out=acc[:],
-                lhsT=words[:, a, cols].bitcast(fmt),
-                lhsT_scale=scales[row:P, a, cols],
-                rhs=x_codes[a][:].bitcast(FP8X4),
-                rhs_scale=x_scales[a][:],
-                start=(a == 0),
-                stop=(a == PASSES - 1),
-            )
+        steps = [(0, 0, JH), (0, JH, J), (1, 0, J), (2, 0, J), (3, 0, J)]
+        gate_ps = [psum.tile([P, j1 - j0], F32, name=f"gate_ps{i}", tag=f"gate_ps{i % 4}") for i, (t, j0, j1) in enumerate(steps[:4])]
+        for i, (t, j0, j1) in enumerate(steps[:4]):
+            product(gate_ps[i], True, t, 0, j0, j1)
 
-        for t in range(PACK):
-            product(gate_ps[t], wg, FP4X4, GATE_ROW, t, 0)
-
-        y = {(u, h): keep.tile([P, 2, HALF], F32, name=f"y{u}{h}") for u in range(2) for h in range(2)}
-        y_grouped = [keep.tile([P, HALF, PACK], BF16, name=f"y_grouped{h}", align_bytes=64) for h in range(2)]
+        y = [keep.tile([P, 4, 2, QUARTER], F32, name="y01")]
+        y_grouped = [keep.tile([P, QUARTER, PACK], BF16, name=f"y_grouped{c}", align_bytes=64) for c in range(4)]
         y_codes = keep.tile([P, T], U32, name="y_codes", align_bytes=64)
         y_scales = keep.tile([P, T], U8, name="y_scales", align_bytes=64)
         out_rows = out_0.rearrange("(p t) c -> p t c", t=PACK)
 
-        for t in range(PACK):
-            product(gate_ps[t], wg, FP4X4, GATE_ROW, t, 1)
-            for a in range(PASSES):
-                product(ans_ps[t], wa, FP8X4, ANSWER_ROW, t, a)
-            gate = keep.tile([P, J], F32, name=f"gate{t}")
-            ans = keep.tile([P, J], F32, name=f"ans{t}")
-            nc.scalar.activation(out=gate[:], in_=gate_ps[t][:], func=ACT.Sigmoid)
-            nc.scalar.activation(out=ans[:], in_=ans_ps[t][:], func=ACT.Copy)
-            nc.vector.tensor_tensor(out=pages[t][:].indirect(offsets[:]), in0=ans[:], in1=gate[:], op=ALU.mult)
+        gated = []
+        for i, (t, j0, j1) in enumerate(steps):
+            if i == 4:
+                gate_ps.append(psum.tile([P, J], F32, name="gate_ps4", tag="gate_ps0"))
+                product(gate_ps[i], True, t, 0, j0, j1)
+            ans_ps = psum.tile([P, j1 - j0], F32, name=f"ans_ps{i}", tag=f"ans_ps{i % 4}")
+            product(ans_ps, False, t, 0, j0, j1)
+            product(gate_ps[i], True, t, 1, j0, j1)
+            product(ans_ps, False, t, 1, j0, j1)
+            gate = keep.tile([P, j1 - j0], F32, name=f"gate{i}")
+            nc.scalar.activation(out=gate[:], in_=gate_ps[i][:], func=ACT.Sigmoid)
+            d = keep.tile([P, j1 - j0], F32, name=f"d{i}")
+            if t == 0:
+                nc.vector.tensor_tensor(out=d[:], in0=ans_ps[:], in1=gate[:], op=ALU.mult)
+            else:
+                ans = keep.tile([P, J], F32, name=f"ans{i}")
+                nc.scalar.activation(out=ans[:], in_=ans_ps[:], func=ACT.Copy)
+                nc.gpsimd.tensor_tensor(out=d[:], in0=ans[:], in1=gate[:], op=ALU.mult)
+            gated.append(d)
+
+        y.append(keep.tile([P, 4, 2, QUARTER], F32, name="y23", tag="gate4"))
+
+        def quarters(ap):
+            return ap.rearrange("p (c w) -> p c w", c=4)
+
+        def round_pair_of_y(engine_copy, u, c):
+            engine_copy(out=y_grouped[c][:, :, 2 * u : 2 * u + 2], in_=y[u][:, c].rearrange("p e w -> p w e"))
+
+        for i, (t, j0, j1) in enumerate(steps):
+            nc.vector.tensor_copy(out=pages[t][:].indirect(offsets[:, j0 // 16 : j1 // 16]), in_=gated[i][:])
+            if j1 < J:
+                continue
             u, e = divmod(t, 2)
-            for h in range(2):
-                cols = slice(h * HALF, (h + 1) * HALF)
-                nc.vector.scalar_tensor_tensor(
-                    out=y[u, h][:, e, :], in0=res_sb[t][:, cols], scalar=0.5, in1=pages[t][:, cols], op0=ALU.mult, op1=ALU.add
-                )
-                nc.sync.dma_start(out=out_rows[:, t, cols], in_=y[u, h][:, e, :])
+            page = quarters(pages[t][:])
+            if t < 3:
+                if t < 2:
+                    half_tile = keep.tile([P, T], F32, name=f"half_res{t}", tag=f"gate{t + 2}")
+                    half_res = quarters(half_tile[:])
+                else:
+                    half_res = y[u][:, :, 1, :]
+                nc.scalar.activation(out=half_res, in_=quarters(res_sb[t][:]), func=ACT.Copy, scale=0.5)
+                for c in (0, 2):
+                    nc.gpsimd.tensor_tensor(
+                        out=y[u][:, c : c + 2, e, :], in0=half_res[:, c : c + 2, :], in1=page[:, c : c + 2, :], op=ALU.add
+                    )
+            else:
+                for c in range(4):
+                    nc.vector.scalar_tensor_tensor(
+                        out=y[u][:, c, e, :], in0=quarters(res_sb[t][:])[:, c, :], scalar=0.5, in1=page[:, c, :], op0=ALU.mult, op1=ALU.add
+                    )
+            nc.sync.dma_start(out=quarters(out_rows[:, t, :]), in_=y[u][:, :, e, :])
             if e == 1:
-                for h in range(2):
-                    src = y[u, h][:].rearrange("p e c -> p c e")
-                    dst = y_grouped[h][:, :, 2 * u : 2 * u + 2]
-                    if u == 1 and h == 1:
-                        nc.vector.tensor_copy(out=dst, in_=src)
-                    else:
-                        nc.scalar.activation(out=dst, in_=src, func=ACT.Copy)
+                for c in range(4 if u == 0 else 3):
+                    round_pair_of_y(nc.scalar.copy, u, c)
 
         code_words = out_1.rearrange("z p c r -> p (z c r)").bitcast(I32)
-        for h in (1, 0):
-            cols = slice(h * HALF, (h + 1) * HALF)
+
+        def quantize_y(c):
+            cols = slice(c * QUARTER, (c + 1) * QUARTER)
             nc.vector.quantize_mx(
-                out=y_codes[:, cols].bitcast(FP8X4), scales=y_scales[:, cols], in_=y_grouped[h][:].rearrange("p c t -> p (c t)")
+                out=y_codes[:, cols].bitcast(FP8X4), scales=y_scales[:, cols], in_=y_grouped[c][:].rearrange("p c t -> p (c t)")
             )
+
+        def store_codes(c0, c1):
+            cols = slice(c0 * QUARTER, c1 * QUARTER)
             nc.sync.dma_start(out=code_words[:, cols], in_=y_codes[:, cols].bitcast(I32))
+
+        quantize_y(0)
+        round_pair_of_y(nc.vector.tensor_copy, 1, 3)
+        quantize_y(1)
+        store_codes(0, 2)
+        for c in (3, 2):
+            quantize_y(c)
+            store_codes(c, c + 1)
         for q in range(4):
-            eng = nc.sync if q % 2 == 0 else nc.scalar
+            eng = nc.scalar if q % 2 == 0 else nc.sync
             eng.dma_start(out=out_2[0, 4 * q : 4 * q + 4, :].bitcast(I32), in_=y_scales[32 * q : 32 * q + 4, :].bitcast(I32))

@@ -34,7 +34,6 @@ def tile_list_expert_self_gate_pl_kernel(tc, xq, wa_words, wa_scales, wg_words, 
         psum = ctx.enter_context(tc.psum_pool(name="psum", bufs=1))
 
         offsets = keep.tile([P, J // 16], U16, name="offsets")
-        nc.sync.dma_start(offsets[:], offs)
 
         scales_raw = keep.tile([P, PASSES, N], U8, name="scales_raw", align_bytes=64)
         nc.gpsimd.memset(scales_raw[:].bitcast(I32), 0)
@@ -60,13 +59,17 @@ def tile_list_expert_self_gate_pl_kernel(tc, xq, wa_words, wa_scales, wg_words, 
         wg_raw = keep.tile([P, PASSES, N], U16, name="wg_raw", align_bytes=64)
         wa_raw = keep.tile([P, PASSES, N], I32, name="wa_raw", align_bytes=64)
         nc.sync.dma_start(out=wg_raw[:].bitcast(I32), in_=wg_words.rearrange("z p b -> p z b").bitcast(I32))
+        nc.sync.dma_start(offsets[:], offs)
         load_x(0, 0, 0)
         load_scales(GATE_ROW, wg_scales)
         load_x(0, 0, 1)
+        load_x(0, 1, 0)
+        load_x(0, 1, 1)
+        load_x(1, 0, 0)
         load_scales(ANSWER_ROW, wa_scales)
-        for a, u in ((0, 1), (1, 0), (1, 1)):
-            for h in range(2):
-                load_x(a, u, h)
+        load_x(1, 0, 1)
+        load_x(1, 1, 0)
+        load_x(1, 1, 1)
         nc.sync.dma_start(out=wa_raw[:], in_=wa_words.rearrange("z p n t -> p z (n t)").bitcast(I32))
         res_rows = res.rearrange("(p t) c -> p t c", t=PACK)
         res_sb = [keep.tile([P, T], F32, name=f"res{t}") for t in range(PACK)]
@@ -78,10 +81,19 @@ def tile_list_expert_self_gate_pl_kernel(tc, xq, wa_words, wa_scales, wg_words, 
         wg = keep.tile([P, PASSES, N], U16, name="wg", align_bytes=64)
         wa = keep.tile([P, PACK, PASSES, P], I32, name="wa", align_bytes=64)
         scales = keep.tile([P, PASSES, N], U8, name="scales", align_bytes=64)
-        for dealt, raw in ((wg, wg_raw), (scales, scales_raw)):
+
+        def deal(dealt, raw):
             nc.vector.tensor_copy(
                 out=dealt[:].rearrange("p z (t q) -> p z t q", t=PACK), in_=raw[:].rearrange("p z (q t) -> p z t q", t=PACK)
             )
+
+        def deal_wa(t0, t1):
+            nc.vector.tensor_copy(
+                out=wa[:, t0:t1].rearrange("p t z (b i) -> p z b t i", i=4),
+                in_=wa_raw[:].rearrange("p z (b i t) -> p z b t i", t=PACK, i=4)[:, :, :, t0:t1, :],
+            )
+
+        deal(wg, wg_raw)
 
         def round_pair(a, u):
             pair = keep.tile([P, T * 2], BF16, name=f"pair{a}{u}", align_bytes=64)
@@ -114,21 +126,20 @@ def tile_list_expert_self_gate_pl_kernel(tc, xq, wa_words, wa_scales, wg_words, 
         for u in range(2):
             gather(picked[0], u, round_pair(0, u), 0, J)
         weave(grouped[0], picked[0], 0, J)
+        deal(scales, scales_raw)
         quantize(0, grouped[0], 0, J)
         gather(picked[1], 0, round_pair(1, 0), 0, J)
         last = round_pair(1, 1)
         halves = ((0, JH), (JH, J))
         for j0, j1 in halves:
             gather(picked[1], 1, last, j0, j1)
-        for j0, j1 in halves:
-            weave(grouped[1], picked[1], j0, j1)
+        weave(grouped[1], picked[1], 0, JH)
+        deal_wa(0, 1)
         quantize(1, grouped[1], 0, JH)
-        nc.vector.tensor_copy(out=wa[:, 0], in_=wa_raw[:].rearrange("p z (q t) -> p t z q", t=PACK)[:, 0])
+        weave(grouped[1], picked[1], JH, J)
+        deal_wa(1, 2)
         quantize(1, grouped[1], JH, J)
-        nc.vector.tensor_copy(
-            out=wa[:, 1:].rearrange("p t z (b i) -> p z b t i", i=4),
-            in_=wa_raw[:].rearrange("p z (b i t) -> p z b t i", t=PACK, i=4)[:, :, :, 1:, :],
-        )
+        deal_wa(2, 4)
 
         def product(acc, gate, t, a, j0, j1):
             width = P if gate and j1 - j0 < J else j1 - j0
@@ -166,10 +177,10 @@ def tile_list_expert_self_gate_pl_kernel(tc, xq, wa_words, wa_scales, wg_words, 
             gate = keep.tile([P, j1 - j0], F32, name=f"gate{i}")
             nc.scalar.activation(out=gate[:], in_=gate_ps[i][:], func=ACT.Sigmoid)
             d = keep.tile([P, j1 - j0], F32, name=f"d{i}")
-            if t == 0:
+            if i == 0:
                 nc.vector.tensor_tensor(out=d[:], in0=ans_ps[:], in1=gate[:], op=ALU.mult)
             else:
-                ans = keep.tile([P, J], F32, name=f"ans{i}")
+                ans = keep.tile([P, j1 - j0], F32, name=f"ans{i}")
                 nc.scalar.activation(out=ans[:], in_=ans_ps[:], func=ACT.Copy)
                 nc.gpsimd.tensor_tensor(out=d[:], in0=ans[:], in1=gate[:], op=ALU.mult)
             gated.append(d)
@@ -195,9 +206,10 @@ def tile_list_expert_self_gate_pl_kernel(tc, xq, wa_words, wa_scales, wg_words, 
                 else:
                     half_res = y[u][:, :, 1, :]
                 nc.scalar.activation(out=half_res, in_=quarters(res_sb[t][:]), func=ACT.Copy, scale=0.5)
-                for c in (0, 2):
+                n = 2 if t == 2 else 4
+                for c in range(0, 4, n):
                     nc.gpsimd.tensor_tensor(
-                        out=y[u][:, c : c + 2, e, :], in0=half_res[:, c : c + 2, :], in1=page[:, c : c + 2, :], op=ALU.add
+                        out=y[u][:, c : c + n, e, :], in0=half_res[:, c : c + n, :], in1=page[:, c : c + n, :], op=ALU.add
                     )
             else:
                 for c in range(4):

from contextlib import ExitStack

import concourse.mybir as mybir

K, T, J, N = 1024, 1024, 512, 512
FLOPS = 2 * 2 * K * N * J

F32 = mybir.dt.float32
BF16 = mybir.dt.bfloat16
I32 = mybir.dt.int32
U32 = mybir.dt.uint32
U16 = mybir.dt.uint16
U8 = mybir.dt.uint8
FP8X4 = mybir.dt.float8_e4m3fn_x4
FP4X4 = mybir.dt.float4_e2m1fn_x4
ALU = mybir.AluOpType
ACT = mybir.ActivationFunctionType

P = 128
PACK = 4
PASSES = K // (P * PACK)
HALF = T // 2
JH = J // 2
QUARTER = T // 4
GATE_ROW = 0
ANSWER_ROW = 4
SCALAR_SHARE = {(0, 0, 1): 320, (0, 1, 1): 256, (1, 1, 1): 256}


def tile_list_expert_self_gate_pl_kernel(tc, xq, wa_words, wa_scales, wg_words, wg_scales, res, offs, out_0, out_1, out_2):
    nc = tc.nc
    with ExitStack() as ctx:
        keep = ctx.enter_context(tc.tile_pool(name="keep", bufs=1))
        psum = ctx.enter_context(tc.psum_pool(name="psum", bufs=1))

        offsets = keep.tile([P, J // 16], U16, name="offsets")

        scales_raw = keep.tile([P, PASSES, N], U8, name="scales_raw", align_bytes=64)
        nc.gpsimd.memset(scales_raw[:].bitcast(I32), 0)

        def load_scales(row, src):
            for q in range(4):
                nc.sync.dma_start(
                    out=scales_raw[32 * q + row : 32 * q + row + 4].bitcast(I32),
                    in_=src[:, 4 * q : 4 * q + 4, :].rearrange("z r c -> r z c").bitcast(I32),
                )

        pages = [keep.tile([P, T], F32, name=f"page{t}") for t in range(PACK)]
        for t in range(PACK):
            nc.vector.memset(pages[t][:], 0.0)

        x_rows = xq.rearrange("(a p i) t -> a p i t", a=PASSES, i=PACK)
        x_raw = {}

        def load_x(a, u, h):
            x_raw[a, u, h] = keep.tile([P, 2, HALF], F32, name=f"x_raw{a}{u}{h}")
            nc.sync.dma_start(out=x_raw[a, u, h][:], in_=x_rows[a, :, 2 * u : 2 * u + 2, h * HALF : (h + 1) * HALF])

        wg_raw = keep.tile([P, PASSES, N], U16, name="wg_raw", align_bytes=64)
        wa_raw = keep.tile([P, PASSES, N], I32, name="wa_raw", align_bytes=64)
        nc.sync.dma_start(out=wg_raw[:].bitcast(I32), in_=wg_words.rearrange("z p b -> p z b").bitcast(I32))
        nc.sync.dma_start(offsets[:], offs)
        load_x(0, 0, 0)
        load_scales(GATE_ROW, wg_scales)
        load_x(0, 0, 1)
        load_x(0, 1, 0)
        load_x(0, 1, 1)
        load_x(1, 0, 0)
        load_scales(ANSWER_ROW, wa_scales)
        load_x(1, 0, 1)
        load_x(1, 1, 0)
        load_x(1, 1, 1)
        nc.sync.dma_start(out=wa_raw[:], in_=wa_words.rearrange("z p n t -> p z (n t)").bitcast(I32))
        res_rows = res.rearrange("(p t) c -> p t c", t=PACK)
        res_sb = [keep.tile([P, T], F32, name=f"res{t}") for t in range(PACK)]
        for t in range(PACK):
            nc.sync.dma_start(out=res_sb[t][:], in_=res_rows[:, t, :])

        x_codes = [keep.tile([P, J], U32, name=f"x_codes{a}", align_bytes=64) for a in range(PASSES)]
        x_scales = [keep.tile([P, J], U8, name=f"x_scales{a}", align_bytes=64) for a in range(PASSES)]
        wg = keep.tile([P, PASSES, N], U16, name="wg", align_bytes=64)
        wa = keep.tile([P, PACK, PASSES, P], I32, name="wa", align_bytes=64)
        scales = keep.tile([P, PASSES, N], U8, name="scales", align_bytes=64)

        def deal(dealt, raw):
            nc.vector.tensor_copy(
                out=dealt[:].rearrange("p z (t q) -> p z t q", t=PACK), in_=raw[:].rearrange("p z (q t) -> p z t q", t=PACK)
            )

        def deal_wa(t0, t1):
            nc.vector.tensor_copy(
                out=wa[:, t0:t1].rearrange("p t z (b i) -> p z b t i", i=4),
                in_=wa_raw[:].rearrange("p z (b i t) -> p z b t i", t=PACK, i=4)[:, :, :, t0:t1, :],
            )

        deal(wg, wg_raw)

        def round_pair(a, u):
            pair = keep.tile([P, T * 2], BF16, name=f"pair{a}{u}", align_bytes=64)
            cols = pair[:].rearrange("p (c e) -> p c e", e=2)
            for h in range(2):
                src = x_raw[a, u, h][:].rearrange("p e c -> p c e")
                dst = cols[:, h * HALF : (h + 1) * HALF, :]
                s = SCALAR_SHARE.get((a, u, h), HALF)
                nc.scalar.activation(out=dst[:, :s, :], in_=src[:, :s, :], func=ACT.Copy)
                if s < HALF:
                    nc.vector.tensor_copy(out=dst[:, s:, :], in_=src[:, s:, :])
            return pair[:].bitcast(F32)

        def gather(picked, u, window, j0, j1):
            nc.vector.tensor_copy(out=picked[:, u, j0:j1], in_=window.indirect(offsets[:, j0 // 16 : j1 // 16]))

        def weave(grouped, picked, j0, j1):
            nc.vector.tensor_copy(
                out=grouped[:, PACK * j0 : PACK * j1].bitcast(F32).rearrange("p (j u) -> p j u", u=2),
                in_=picked[:, :, j0:j1].rearrange("p u j -> p j u"),
            )

        def quantize(a, grouped, j0, j1):
            nc.vector.quantize_mx(
                out=x_codes[a][:, j0:j1].bitcast(FP8X4), scales=x_scales[a][:, j0:j1], in_=grouped[:, PACK * j0 : PACK * j1]
            )

        picked = [keep.tile([P, 2, J], F32, name=f"picked{a}") for a in range(PASSES)]
        grouped = [keep.tile([P, J * PACK], BF16, name=f"grouped{a}", align_bytes=64) for a in range(PASSES)]
        for u in range(2):
            gather(picked[0], u, round_pair(0, u), 0, J)
        weave(grouped[0], picked[0], 0, J)
        deal(scales, scales_raw)
        quantize(0, grouped[0], 0, J)
        gather(picked[1], 0, round_pair(1, 0), 0, J)
        last = round_pair(1, 1)
        halves = ((0, JH), (JH, J))
        for j0, j1 in halves:
            gather(picked[1], 1, last, j0, j1)
        weave(grouped[1], picked[1], 0, JH)
        deal_wa(0, 1)
        quantize(1, grouped[1], 0, JH)
        weave(grouped[1], picked[1], JH, J)
        deal_wa(1, 2)
        quantize(1, grouped[1], JH, J)
        deal_wa(2, 4)

        def product(acc, gate, t, a, j0, j1):
            width = P if gate and j1 - j0 < J else j1 - j0
            for c in range(j0, j1, width):
                nc.tensor.matmul_mx(
                    out=acc[:, c - j0 : c - j0 + width],
                    lhsT=wg[:, a, t * P : (t + 1) * P].bitcast(FP4X4) if gate else wa[:, t, a, :].bitcast(FP8X4),
                    lhsT_scale=scales[(GATE_ROW if gate else ANSWER_ROW) : P, a, t * P : (t + 1) * P],
                    rhs=x_codes[a][:, c : c + width].bitcast(FP8X4),
                    rhs_scale=x_scales[a][:, c : c + width],
                    start=(a == 0 and c == j0),
                    stop=(a == PASSES - 1 and c + width == j1),
                )

        steps = [(0, 0, JH), (0, JH, J), (1, 0, J), (2, 0, J), (3, 0, J)]
        gate_ps = [psum.tile([P, j1 - j0], F32, name=f"gate_ps{i}", tag=f"gate_ps{i % 4}") for i, (t, j0, j1) in enumerate(steps[:4])]
        for i, (t, j0, j1) in enumerate(steps[:4]):
            product(gate_ps[i], True, t, 0, j0, j1)

        y = [keep.tile([P, 4, 2, QUARTER], F32, name="y01")]
        y_grouped = [keep.tile([P, QUARTER, PACK], BF16, name=f"y_grouped{c}", align_bytes=64) for c in range(4)]
        y_codes = keep.tile([P, T], U32, name="y_codes", align_bytes=64)
        y_scales = keep.tile([P, T], U8, name="y_scales", align_bytes=64)
        out_rows = out_0.rearrange("(p t) c -> p t c", t=PACK)

        gated = []
        for i, (t, j0, j1) in enumerate(steps):
            if i == 4:
                gate_ps.append(psum.tile([P, J], F32, name="gate_ps4", tag="gate_ps0"))
                product(gate_ps[i], True, t, 0, j0, j1)
            ans_ps = psum.tile([P, j1 - j0], F32, name=f"ans_ps{i}", tag=f"ans_ps{i % 4}")
            product(ans_ps, False, t, 0, j0, j1)
            product(gate_ps[i], True, t, 1, j0, j1)
            product(ans_ps, False, t, 1, j0, j1)
            gate = keep.tile([P, j1 - j0], F32, name=f"gate{i}")
            nc.scalar.activation(out=gate[:], in_=gate_ps[i][:], func=ACT.Sigmoid)
            d = keep.tile([P, j1 - j0], F32, name=f"d{i}")
            if i == 0:
                nc.vector.tensor_tensor(out=d[:], in0=ans_ps[:], in1=gate[:], op=ALU.mult)
            else:
                ans = keep.tile([P, j1 - j0], F32, name=f"ans{i}")
                nc.scalar.activation(out=ans[:], in_=ans_ps[:], func=ACT.Copy)
                nc.gpsimd.tensor_tensor(out=d[:], in0=ans[:], in1=gate[:], op=ALU.mult)
            gated.append(d)

        y.append(keep.tile([P, 4, 2, QUARTER], F32, name="y23", tag="gate4"))

        def quarters(ap):
            return ap.rearrange("p (c w) -> p c w", c=4)

        def round_pair_of_y(engine_copy, u, c):
            engine_copy(out=y_grouped[c][:, :, 2 * u : 2 * u + 2], in_=y[u][:, c].rearrange("p e w -> p w e"))

        for i, (t, j0, j1) in enumerate(steps):
            nc.vector.tensor_copy(out=pages[t][:].indirect(offsets[:, j0 // 16 : j1 // 16]), in_=gated[i][:])
            if j1 < J:
                continue
            u, e = divmod(t, 2)
            page = quarters(pages[t][:])
            if t < 3:
                if t < 2:
                    half_tile = keep.tile([P, T], F32, name=f"half_res{t}", tag=f"gate{t + 2}")
                    half_res = quarters(half_tile[:])
                else:
                    half_res = y[u][:, :, 1, :]
                nc.scalar.activation(out=half_res, in_=quarters(res_sb[t][:]), func=ACT.Copy, scale=0.5)
                n = 2 if t == 2 else 4
                for c in range(0, 4, n):
                    nc.gpsimd.tensor_tensor(
                        out=y[u][:, c : c + n, e, :], in0=half_res[:, c : c + n, :], in1=page[:, c : c + n, :], op=ALU.add
                    )
            else:
                for c in range(4):
                    nc.vector.scalar_tensor_tensor(
                        out=y[u][:, c, e, :], in0=quarters(res_sb[t][:])[:, c, :], scalar=0.5, in1=page[:, c, :], op0=ALU.mult, op1=ALU.add
                    )
            nc.sync.dma_start(out=quarters(out_rows[:, t, :]), in_=y[u][:, :, e, :])
            if e == 1:
                for c in range(4 if u == 0 else 3):
                    round_pair_of_y(nc.scalar.copy, u, c)

        code_words = out_1.rearrange("z p c r -> p (z c r)").bitcast(I32)

        def quantize_y(c):
            cols = slice(c * QUARTER, (c + 1) * QUARTER)
            nc.vector.quantize_mx(
                out=y_codes[:, cols].bitcast(FP8X4), scales=y_scales[:, cols], in_=y_grouped[c][:].rearrange("p c t -> p (c t)")
            )

        def store_codes(c0, c1):
            cols = slice(c0 * QUARTER, c1 * QUARTER)
            nc.sync.dma_start(out=code_words[:, cols], in_=y_codes[:, cols].bitcast(I32))

        quantize_y(0)
        round_pair_of_y(nc.vector.tensor_copy, 1, 3)
        quantize_y(1)
        store_codes(0, 2)
        for c in (3, 2):
            quantize_y(c)
            store_codes(c, c + 1)
        for q in range(4):
            eng = nc.scalar if q % 2 == 0 else nc.sync
            eng.dma_start(out=out_2[0, 4 * q : 4 * q + 4, :].bitcast(I32), in_=y_scales[32 * q : 32 * q + 4, :].bitcast(I32))
